import numpy as np
CORES = [5,21,45,77,85,101,109,125,133,141,189,213]
N = 12
F = 64
LR = 0.5
def setup_inputs(rng):
    return {"w": rng.standard_normal((N, 128, F), dtype=np.float32) * (0.5 + np.abs(rng.standard_normal((N, 128, 1), dtype=np.float32))), "u": rng.standard_normal((N, 128, F), dtype=np.float32) * (0.5 + np.abs(rng.standard_normal((N, 128, 1), dtype=np.float32)))}
def setup_inputs_big(rng):
    d = setup_inputs(rng)
    for k in ("w", "u"): d[k] = (d[k].astype(np.float32) * 1024.0).astype(d[k].dtype)
    return d
def setup_inputs_small(rng):
    d = setup_inputs(rng)
    for k in ("w", "u"): d[k] = (d[k].astype(np.float32) * (1 / 1024.0)).astype(d[k].dtype)
    return d
def setup_inputs_apart(rng):
    d = setup_inputs(rng)
    f = (10.0 ** rng.permutation(np.linspace(-1.5, 1.5, N))).astype(np.float32).reshape(N, 1, 1)
    for k in ("w", "u"): d[k] = (d[k].astype(np.float32) * f).astype(d[k].dtype)
    return d
def setup_inputs_mixed(rng):
    d = setup_inputs(rng)
    f = (10.0 ** rng.uniform(-3, 3, (1, 128, 1))).astype(np.float32); shape = rng.integers(3, size=(1, 128, 1))
    for k in ("u",):
        x = d[k].astype(np.float32)
        m = x.mean(axis=(0, 2), keepdims=True); level = m + np.sign(x - m) * np.abs(x - m).mean(axis=(0, 2), keepdims=True) * rng.uniform(0.9, 1.1, x.shape).astype(np.float32)
        other = x * np.where(rng.random(x.shape) < 0.5, 0.1, 1.0).astype(np.float32)
        d[k] = (np.where(shape == 1, level, np.where(shape == 2, other, x)) * f).astype(d[k].dtype)
    return d
def reference(w, u):
    W, U = w.astype(np.float64), u.astype(np.float64)
    nw = np.sqrt((W ** 2).sum(axis=(0, 2)).reshape(1, 128, 1))
    nu = np.sqrt((U ** 2).sum(axis=(0, 2)).reshape(1, 128, 1))
    return {"y": (W - LR * (nw / nu) * U).astype(np.float32)}

@@ -1,0 +1,127 @@
+from concourse.bass import DstId, RemoteDMATransfer
+from concourse.mybir import AluOpType, AxisListType, ActivationFunctionType
+
+F = 64
+RELAYS = 2
+E_CHIP = 8
+E_PLANE = 8
+E_RELAY = 8
+OWN = 4
+
+SCRATCH = {
+    "wb": ("sbuf", [128, F], "float32"),
+    "ub": ("sbuf", [128, F], "float32"),
+    "sq": ("sbuf", [128, 2 * F], "float32"),
+    "land": ("sbuf", [128, 28], "float32"),
+    "x": ("sbuf", [128, 2], "float32"),
+    "s": ("sbuf", [128, 2], "float32"),
+    "r": ("sbuf", [128, 2], "float32"),
+    "nt": ("sbuf", [128, 4], "float32"),
+    "tp": ("psum", [128, F], "float32"),
+    "yb": ("sbuf", [128, F], "float32"),
+}
+SEMAPHORES = ["ldw", "ldu", "sums", "sent", "handed", "arrived", "vec", "root", "done", "stored"]
+
+
+def _pick(mask, k):
+    out = 0
+    for b in [b for b in range(mask.bit_length()) if (mask >> b) & 1][:k]:
+        out |= 1 << b
+    return out
+
+
+def _plan(T, topo):
+    cores = list(T.cores)
+    world = range((1 + max(topo.host(c) for c in cores)) * topo.CORES_PER_HOST)
+    plan = {}
+    for c in cores:
+        near = [d for d in cores if d != c and topo.may_write(c, d)]
+        far = [d for d in cores if d != c and not topo.may_write(c, d)]
+        able = [k for k in world if k not in cores and topo.host(k) == topo.host(c) and topo.chip(k) == topo.chip(c)
+                and all(topo.may_write(k, d) for d in far)]
+        able.sort(key=lambda k: (topo.die(k) != topo.die(c), k))
+        n = min(RELAYS, len(far))
+        plan[c] = (near, [(able[i], far[i::n]) for i in range(n)])
+    return plan
+
+
+def _write(g, topo, core, src, dests, engines, remote_sem, local_sem):
+    mask = topo.mask(core, dests[0][0])
+    for d, _ in dests:
+        mask &= topo.mask(core, d)
+    ids = []
+    for d, _ in dests:
+        rid, pid = topo.addr(d, core)
+        ids.append(DstId(rid=rid, pnc=pid))
+    g.remote_dma_fused([RemoteDMATransfer(dst_ids=ids, dma_engine_mask=_pick(mask, engines), remote_sem=remote_sem,
+                                          srcs=[src], dsts=[ap for _, ap in dests], alu_op=0)], local_sem=local_sem)
+
+
+def rank_program(g, core, T, topo):
+    plan = _plan(T, topo)
+    sem = T.sem
+    pair = T.land[:, 0:2]
+
+    def slot(dst, src):
+        a, b = T.rank_of(src), T.rank_of(dst)
+        col = OWN + 2 * (a if a < b else a - 1)
+        return T.land[:, col:col + 2]
+
+    if T.rank_of(core) is None:
+        for c, (_, relays) in plan.items():
+            for k, share in relays:
+                if k == core:
+                    g.wait_ge(sem.handed, E_CHIP)
+                    _write(g, topo, core, pair, [(d, slot(d, c)) for d in share], E_RELAY, sem.arrived, sem.sent)
+                    g.wait_ge(sem.sent, E_RELAY)
+        return
+
+    near, relays = plan[core]
+    mult, add, sub = AluOpType.mult, AluOpType.add, AluOpType.subtract
+    Act = ActivationFunctionType
+    v, sc, sy = g.vector, g.scalar, g.sync
+
+    sy.dma_start(T.wb[:], T.w[:]).then_inc(sem.ldw, 16)
+    sc.dma_start(T.ub[:], T.u[:]).then_inc(sem.ldu, 16)
+    v.memset(T.land[:, 2:OWN], 0.0).then_inc(sem.vec, 1)
+    sc.wait_ge(sem.ldw, 16)
+    sc.activation(T.sq[:, 0:F], T.wb[:], Act.Square, scale=0.25, accum_out=T.land[:, 0:1]).then_inc(sem.sums, 1)
+    sc.wait_ge(sem.ldu, 16)
+    sc.activation(T.sq[:, F:2 * F], T.ub[:], Act.Square, accum_out=T.land[:, 1:2]).then_inc(sem.sums, 1)
+
+    g.wait_ge(sem.sums, 2)
+    left = 0
+    if relays:
+        _write(g, topo, core, pair, [(k, pair) for k, _ in relays], E_CHIP, sem.handed, sem.sent)
+        left += E_CHIP
+    if near:
+        _write(g, topo, core, pair, [(d, slot(d, core)) for d in near], E_PLANE, sem.arrived, sem.sent)
+        left += E_PLANE
+
+    due = sum(E_PLANE if core in plan[c][0] else E_RELAY for c in T.cores if c != core)
+    end = OWN + 2 * (len(T.cores) - 1)
+    v.wait_ge(sem.vec, 1)
+    v.wait_ge(sem.ldw, 16)
+    v.wait_ge(sem.ldu, 16)
+    v.wait_ge(sem.sums, 2)
+    v.wait_ge(sem.arrived, due)
+    v.tensor_reduce(T.x[:, 0:1], T.land[:, 0:end:2], AxisListType.X, add).then_inc(sem.vec, 1)
+    v.tensor_reduce(T.x[:, 1:2], T.land[:, 1:end:2], AxisListType.X, add).then_inc(sem.vec, 1)
+    sc.wait_ge(sem.vec, 3)
+    sc.activation(T.s[:], T.x[:], Act.Sqrt).then_inc(sem.root, 1)
+    v.wait_ge(sem.root, 1)
+    v.reciprocal(T.r[:], T.s[:]).then_inc(sem.vec, 1)
+    v.wait_ge(sem.vec, 4)
+    v.tensor_scalar(T.nt[:, 0:1], T.x[:, 1:2], T.r[:, 1:2], T.r[:, 1:2], mult, mult).then_inc(sem.vec, 1)
+    v.tensor_scalar(T.nt[:, 1:2], T.x[:, 0:1], T.r[:, 0:1], T.s[:, 0:1], mult, add).then_inc(sem.vec, 1)
+    v.wait_ge(sem.vec, 6)
+    v.tensor_scalar(T.nt[:, 2:3], T.nt[:, 0:1], -0.5, 1.5, mult, add).then_inc(sem.vec, 1)
+    v.tensor_scalar(T.nt[:, 3:4], T.nt[:, 1:2], T.r[:, 1:2], None, mult).then_inc(sem.vec, 1)
+    v.wait_ge(sem.vec, 8)
+    v.tensor_scalar(T.tp[:], T.ub[:], T.nt[:, 2:3], T.nt[:, 3:4], mult, mult).then_inc(sem.vec, 1)
+    v.wait_ge(sem.vec, 9)
+    v.tensor_tensor(T.yb[:], T.wb[:], T.tp[:], sub).then_inc(sem.done, 1)
+    sy.wait_ge(sem.done, 1)
+    sy.dma_start(T.y[:], T.yb[:]).then_inc(sem.stored, 16)
+    sy.wait_ge(sem.stored, 16)
+    g.wait_ge(sem.sent, left)

@@ -13,14 +13,14 @@ SCRATCH = {
     "ub": ("sbuf", [128, F], "float32"),
     "sq": ("sbuf", [128, 2 * F], "float32"),
     "land": ("sbuf", [128, 28], "float32"),
-    "x": ("sbuf", [128, 2], "float32"),
-    "s": ("sbuf", [128, 2], "float32"),
-    "r": ("sbuf", [128, 2], "float32"),
-    "nt": ("sbuf", [128, 4], "float32"),
+    "gs": ("sbuf", [128, 8], "float32"),
+    "kr": ("sbuf", [128, 2], "float32"),
+    "sc": ("sbuf", [128, 16], "float32"),
+    "fin": ("sbuf", [128, 5], "float32"),
     "tp": ("psum", [128, F], "float32"),
     "yb": ("sbuf", [128, F], "float32"),
 }
-SEMAPHORES = ["ldw", "ldu", "sums", "sent", "handed", "arrived", "vec", "root", "done", "stored"]
+SEMAPHORES = ["ldw", "ldu", "sums", "sent", "handed", "arrived", "vec", "guess", "xk", "root", "done", "stored"]
 
 
 def _pick(mask, k):
@@ -85,7 +85,7 @@ def rank_program(g, core, T, topo):
     sc.dma_start(T.ub[:], T.u[:]).then_inc(sem.ldu, 16)
     v.memset(T.land[:, 2:OWN], 0.0).then_inc(sem.vec, 1)
     sc.wait_ge(sem.ldw, 16)
-    sc.activation(T.sq[:, 0:F], T.wb[:], Act.Square, scale=0.25, accum_out=T.land[:, 0:1]).then_inc(sem.sums, 1)
+    sc.activation(T.sq[:, 0:F], T.wb[:], Act.Square, scale=0.5, accum_out=T.land[:, 0:1]).then_inc(sem.sums, 1)
     sc.wait_ge(sem.ldu, 16)
     sc.activation(T.sq[:, F:2 * F], T.ub[:], Act.Square, accum_out=T.land[:, 1:2]).then_inc(sem.sums, 1)
 
@@ -98,28 +98,42 @@ def rank_program(g, core, T, topo):
         _write(g, topo, core, pair, [(d, slot(d, core)) for d in near], E_PLANE, sem.arrived, sem.sent)
         left += E_PLANE
 
-    due = sum(E_PLANE if core in plan[c][0] else E_RELAY for c in T.cores if c != core)
-    end = OWN + 2 * (len(T.cores) - 1)
+    kap, rho = T.kr[:, 0:1], T.kr[:, 1:2]
     v.wait_ge(sem.vec, 1)
+    v.wait_ge(sem.sums, 2)
+    v.tensor_scalar(T.gs[:, 0:2], pair, 0.0, None, AluOpType.is_equal).then_inc(sem.vec, 1)
+    v.wait_ge(sem.vec, 2)
+    v.tensor_tensor(T.gs[:, 2:4], pair, T.gs[:, 0:2], add).then_inc(sem.vec, 1)
+    sc.wait_ge(sem.vec, 3)
+    sc.activation(T.gs[:, 4:6], T.gs[:, 2:4], Act.Sqrt).then_inc(sem.guess, 1)
+    v.wait_ge(sem.guess, 1)
+    v.reciprocal(T.gs[:, 6:8], T.gs[:, 4:6]).then_inc(sem.vec, 1)
+    v.wait_ge(sem.vec, 4)
+    v.tensor_scalar(kap, T.gs[:, 5:6], T.gs[:, 6:7], None, mult).then_inc(sem.vec, 1)
+    v.tensor_scalar(rho, T.gs[:, 4:5], T.gs[:, 7:8], None, mult).then_inc(sem.vec, 1)
+    v.wait_ge(sem.vec, 6)
     v.wait_ge(sem.ldw, 16)
     v.wait_ge(sem.ldu, 16)
-    v.wait_ge(sem.sums, 2)
+
+    due = sum(E_PLANE if core in plan[c][0] else E_RELAY for c in T.cores if c != core)
+    end = OWN + 2 * (len(T.cores) - 1)
+    n = len(range(0, end, 2))
+    xk, usum, urec, q, rq = (T.fin[:, i:i + 1] for i in range(5))
+    sc.wait_ge(sem.vec, 6)
+    sc.wait_ge(sem.arrived, due)
+    sc.activation(T.sc[:, 0:n], T.land[:, 0:end:2], Act.Identity, scale=kap, accum_out=xk).then_inc(sem.xk, 1)
     v.wait_ge(sem.arrived, due)
-    v.tensor_reduce(T.x[:, 0:1], T.land[:, 0:end:2], AxisListType.X, add).then_inc(sem.vec, 1)
-    v.tensor_reduce(T.x[:, 1:2], T.land[:, 1:end:2], AxisListType.X, add).then_inc(sem.vec, 1)
-    sc.wait_ge(sem.vec, 3)
-    sc.activation(T.s[:], T.x[:], Act.Sqrt).then_inc(sem.root, 1)
-    v.wait_ge(sem.root, 1)
-    v.reciprocal(T.r[:], T.s[:]).then_inc(sem.vec, 1)
-    v.wait_ge(sem.vec, 4)
-    v.tensor_scalar(T.nt[:, 0:1], T.x[:, 1:2], T.r[:, 1:2], T.r[:, 1:2], mult, mult).then_inc(sem.vec, 1)
-    v.tensor_scalar(T.nt[:, 1:2], T.x[:, 0:1], T.r[:, 0:1], T.s[:, 0:1], mult, add).then_inc(sem.vec, 1)
-    v.wait_ge(sem.vec, 6)
-    v.tensor_scalar(T.nt[:, 2:3], T.nt[:, 0:1], -0.5, 1.5, mult, add).then_inc(sem.vec, 1)
-    v.tensor_scalar(T.nt[:, 3:4], T.nt[:, 1:2], T.r[:, 1:2], None, mult).then_inc(sem.vec, 1)
+    v.tensor_reduce(usum, T.land[:, 1:end:2], AxisListType.X, add).then_inc(sem.vec, 1)
+    v.wait_ge(sem.vec, 7)
+    v.reciprocal(urec, usum).then_inc(sem.vec, 1)
     v.wait_ge(sem.vec, 8)
-    v.tensor_scalar(T.tp[:], T.ub[:], T.nt[:, 2:3], T.nt[:, 3:4], mult, mult).then_inc(sem.vec, 1)
-    v.wait_ge(sem.vec, 9)
+    v.wait_ge(sem.xk, 1)
+    v.tensor_scalar(q, urec, kap, xk, mult, mult).then_inc(sem.vec, 1)
+    sc.wait_ge(sem.vec, 9)
+    sc.activation(rq, q, Act.Sqrt).then_inc(sem.root, 1)
+    v.wait_ge(sem.root, 1)
+    v.tensor_scalar(T.tp[:], T.ub[:], rq, rho, mult, mult).then_inc(sem.vec, 1)
+    v.wait_ge(sem.vec, 10)
     v.tensor_tensor(T.yb[:], T.wb[:], T.tp[:], sub).then_inc(sem.done, 1)
     sy.wait_ge(sem.done, 1)
     sy.dma_start(T.y[:], T.yb[:]).then_inc(sem.stored, 16)

@@ -1,5 +1,5 @@
 from concourse.bass import DstId, RemoteDMATransfer
-from concourse.mybir import AluOpType, AxisListType, ActivationFunctionType
+from concourse.mybir import AluOpType, ActivationFunctionType
 
 F = 64
 RELAYS = 2
@@ -7,16 +7,21 @@ E_CHIP = 8
 E_PLANE = 8
 E_RELAY = 8
 OWN = 4
+SHIFT = 2.0 ** -20
 
 SCRATCH = {
     "wb": ("sbuf", [128, F], "float32"),
     "ub": ("sbuf", [128, F], "float32"),
     "sq": ("sbuf", [128, 2 * F], "float32"),
     "land": ("sbuf", [128, 28], "float32"),
-    "gs": ("sbuf", [128, 8], "float32"),
+    "gs": ("sbuf", [128, 6], "float32"),
+    "iv": ("sbuf", [128, 4], "float32"),
     "kr": ("sbuf", [128, 2], "float32"),
-    "sc": ("sbuf", [128, 16], "float32"),
-    "fin": ("sbuf", [128, 5], "float32"),
+    "dd": ("sbuf", [128, 16], "float32"),
+    "ur": ("sbuf", [128, F], "float32"),
+    "sa": ("sbuf", [128, 16], "float32"),
+    "sb": ("sbuf", [128, 16], "float32"),
+    "fin": ("sbuf", [128, 4], "float32"),
     "tp": ("psum", [128, F], "float32"),
     "yb": ("sbuf", [128, F], "float32"),
 }
@@ -80,10 +85,18 @@ def rank_program(g, core, T, topo):
     mult, add, sub = AluOpType.mult, AluOpType.add, AluOpType.subtract
     Act = ActivationFunctionType
     v, sc, sy = g.vector, g.scalar, g.sync
+    end = OWN + 2 * (len(T.cores) - 1)
+    n = len(range(0, end, 2))
+    nv = [0]
+
+    def vec(inst):
+        inst.then_inc(sem.vec, 1)
+        nv[0] += 1
 
     sy.dma_start(T.wb[:], T.w[:]).then_inc(sem.ldw, 16)
     sc.dma_start(T.ub[:], T.u[:]).then_inc(sem.ldu, 16)
-    v.memset(T.land[:, 2:OWN], 0.0).then_inc(sem.vec, 1)
+    vec(v.memset(T.land[:, 2:OWN], 0.0))
+    vec(v.memset(T.dd[:, 0:n - 1], 1.0))
     sc.wait_ge(sem.ldw, 16)
     sc.activation(T.sq[:, 0:F], T.wb[:], Act.Square, scale=0.5, accum_out=T.land[:, 0:1]).then_inc(sem.sums, 1)
     sc.wait_ge(sem.ldu, 16)
@@ -98,42 +111,44 @@ def rank_program(g, core, T, topo):
         _write(g, topo, core, pair, [(d, slot(d, core)) for d in near], E_PLANE, sem.arrived, sem.sent)
         left += E_PLANE
 
-    kap, rho = T.kr[:, 0:1], T.kr[:, 1:2]
-    v.wait_ge(sem.vec, 1)
+    a, rho = T.kr[:, 0:1], T.kr[:, 1:2]
+    v.wait_ge(sem.vec, nv[0])
     v.wait_ge(sem.sums, 2)
-    v.tensor_scalar(T.gs[:, 0:2], pair, 0.0, None, AluOpType.is_equal).then_inc(sem.vec, 1)
-    v.wait_ge(sem.vec, 2)
-    v.tensor_tensor(T.gs[:, 2:4], pair, T.gs[:, 0:2], add).then_inc(sem.vec, 1)
-    sc.wait_ge(sem.vec, 3)
+    vec(v.tensor_scalar(T.gs[:, 0:2], pair, 0.0, None, AluOpType.is_equal))
+    v.wait_ge(sem.vec, nv[0])
+    vec(v.tensor_tensor(T.gs[:, 2:4], pair, T.gs[:, 0:2], add))
+    sc.wait_ge(sem.vec, nv[0])
     sc.activation(T.gs[:, 4:6], T.gs[:, 2:4], Act.Sqrt).then_inc(sem.guess, 1)
+    v.wait_ge(sem.vec, nv[0])
     v.wait_ge(sem.guess, 1)
-    v.reciprocal(T.gs[:, 6:8], T.gs[:, 4:6]).then_inc(sem.vec, 1)
-    v.wait_ge(sem.vec, 4)
-    v.tensor_scalar(kap, T.gs[:, 5:6], T.gs[:, 6:7], None, mult).then_inc(sem.vec, 1)
-    v.tensor_scalar(rho, T.gs[:, 4:5], T.gs[:, 7:8], None, mult).then_inc(sem.vec, 1)
-    v.wait_ge(sem.vec, 6)
-    v.wait_ge(sem.ldw, 16)
+    vec(v.reciprocal(T.iv[:], T.gs[:, 2:6]))
+    v.wait_ge(sem.vec, nv[0])
+    vec(v.tensor_scalar(a, T.iv[:, 0:1], SHIFT, None, mult))
+    vec(v.tensor_scalar(T.dd[:, n - 1:n], T.iv[:, 1:2], SHIFT, None, mult))
+    vec(v.tensor_scalar(rho, T.gs[:, 4:5], T.iv[:, 3:4], None, mult))
+    sc.wait_ge(sem.vec, nv[0])
+    v.wait_ge(sem.vec, nv[0])
     v.wait_ge(sem.ldu, 16)
+    vec(v.tensor_scalar(T.ur[:], T.ub[:], rho, None, mult))
+    v.wait_ge(sem.vec, nv[0])
+    v.wait_ge(sem.ldw, 16)
 
     due = sum(E_PLANE if core in plan[c][0] else E_RELAY for c in T.cores if c != core)
-    end = OWN + 2 * (len(T.cores) - 1)
-    n = len(range(0, end, 2))
-    xk, usum, urec, q, rq = (T.fin[:, i:i + 1] for i in range(5))
-    sc.wait_ge(sem.vec, 6)
+    big_a, rt, rec = (T.fin[:, i:i + 1] for i in range(3))
+    big_b = T.sb[:, n - 1:n]
     sc.wait_ge(sem.arrived, due)
-    sc.activation(T.sc[:, 0:n], T.land[:, 0:end:2], Act.Identity, scale=kap, accum_out=xk).then_inc(sem.xk, 1)
+    sc.activation(T.sa[:, 0:n], T.land[:, 0:end:2], Act.Identity, scale=a, accum_out=big_a).then_inc(sem.xk, 1)
     v.wait_ge(sem.arrived, due)
-    v.tensor_reduce(usum, T.land[:, 1:end:2], AxisListType.X, add).then_inc(sem.vec, 1)
-    v.wait_ge(sem.vec, 7)
-    v.reciprocal(urec, usum).then_inc(sem.vec, 1)
-    v.wait_ge(sem.vec, 8)
-    v.wait_ge(sem.xk, 1)
-    v.tensor_scalar(q, urec, kap, xk, mult, mult).then_inc(sem.vec, 1)
-    sc.wait_ge(sem.vec, 9)
-    sc.activation(rq, q, Act.Sqrt).then_inc(sem.root, 1)
+    vec(v.tensor_tensor_scan(T.sb[:, 0:n], T.land[:, 1:end:2], T.dd[:, 0:n], 0.0, add, mult))
+    sc.wait_ge(sem.xk, 1)
+    sc.wait_ge(sem.vec, nv[0])
+    sc.activation(rt, big_b, Act.Sqrt, scale=big_a).then_inc(sem.root, 1)
+    v.wait_ge(sem.vec, nv[0])
+    vec(v.reciprocal(rec, big_b))
+    v.wait_ge(sem.vec, nv[0])
     v.wait_ge(sem.root, 1)
-    v.tensor_scalar(T.tp[:], T.ub[:], rq, rho, mult, mult).then_inc(sem.vec, 1)
-    v.wait_ge(sem.vec, 10)
+    vec(v.tensor_scalar(T.tp[:], T.ur[:], rt, rec, mult, mult))
+    v.wait_ge(sem.vec, nv[0])
     v.tensor_tensor(T.yb[:], T.wb[:], T.tp[:], sub).then_inc(sem.done, 1)
     sy.wait_ge(sem.done, 1)
     sy.dma_start(T.y[:], T.yb[:]).then_inc(sem.stored, 16)

from concourse.bass import DstId, RemoteDMATransfer
from concourse.mybir import AluOpType, ActivationFunctionType

F = 64
RELAYS = 2
E_CHIP = 8
E_PLANE = 8
E_RELAY = 8
OWN = 4
SHIFT = 2.0 ** -20

SCRATCH = {
    "wb": ("sbuf", [128, F], "float32"),
    "ub": ("sbuf", [128, F], "float32"),
    "sq": ("sbuf", [128, 2 * F], "float32"),
    "land": ("sbuf", [128, 28], "float32"),
    "gs": ("sbuf", [128, 6], "float32"),
    "iv": ("sbuf", [128, 4], "float32"),
    "kr": ("sbuf", [128, 2], "float32"),
    "dd": ("sbuf", [128, 16], "float32"),
    "ur": ("sbuf", [128, F], "float32"),
    "sa": ("sbuf", [128, 16], "float32"),
    "sb": ("sbuf", [128, 16], "float32"),
    "fin": ("sbuf", [128, 4], "float32"),
    "tp": ("psum", [128, F], "float32"),
    "yb": ("sbuf", [128, F], "float32"),
}
SEMAPHORES = ["ldw", "ldu", "sums", "sent", "handed", "arrived", "vec", "guess", "xk", "root", "done", "stored"]


def _pick(mask, k):
    out = 0
    for b in [b for b in range(mask.bit_length()) if (mask >> b) & 1][:k]:
        out |= 1 << b
    return out


def _plan(T, topo):
    cores = list(T.cores)
    world = range((1 + max(topo.host(c) for c in cores)) * topo.CORES_PER_HOST)
    plan = {}
    for c in cores:
        near = [d for d in cores if d != c and topo.may_write(c, d)]
        far = [d for d in cores if d != c and not topo.may_write(c, d)]
        able = [k for k in world if k not in cores and topo.host(k) == topo.host(c) and topo.chip(k) == topo.chip(c)
                and all(topo.may_write(k, d) for d in far)]
        able.sort(key=lambda k: (topo.die(k) != topo.die(c), k))
        n = min(RELAYS, len(far))
        plan[c] = (near, [(able[i], far[i::n]) for i in range(n)])
    return plan


def _write(g, topo, core, src, dests, engines, remote_sem, local_sem):
    mask = topo.mask(core, dests[0][0])
    for d, _ in dests:
        mask &= topo.mask(core, d)
    ids = []
    for d, _ in dests:
        rid, pid = topo.addr(d, core)
        ids.append(DstId(rid=rid, pnc=pid))
    g.remote_dma_fused([RemoteDMATransfer(dst_ids=ids, dma_engine_mask=_pick(mask, engines), remote_sem=remote_sem,
                                          srcs=[src], dsts=[ap for _, ap in dests], alu_op=0)], local_sem=local_sem)


def rank_program(g, core, T, topo):
    plan = _plan(T, topo)
    sem = T.sem
    pair = T.land[:, 0:2]

    def slot(dst, src):
        a, b = T.rank_of(src), T.rank_of(dst)
        col = OWN + 2 * (a if a < b else a - 1)
        return T.land[:, col:col + 2]

    if T.rank_of(core) is None:
        for c, (_, relays) in plan.items():
            for k, share in relays:
                if k == core:
                    g.wait_ge(sem.handed, E_CHIP)
                    _write(g, topo, core, pair, [(d, slot(d, c)) for d in share], E_RELAY, sem.arrived, sem.sent)
                    g.wait_ge(sem.sent, E_RELAY)
        return

    near, relays = plan[core]
    mult, add, sub = AluOpType.mult, AluOpType.add, AluOpType.subtract
    Act = ActivationFunctionType
    v, sc, sy = g.vector, g.scalar, g.sync
    end = OWN + 2 * (len(T.cores) - 1)
    n = len(range(0, end, 2))
    nv = [0]

    def vec(inst):
        inst.then_inc(sem.vec, 1)
        nv[0] += 1

    sy.dma_start(T.wb[:], T.w[:]).then_inc(sem.ldw, 16)
    sc.dma_start(T.ub[:], T.u[:]).then_inc(sem.ldu, 16)
    vec(v.memset(T.land[:, 2:OWN], 0.0))
    vec(v.memset(T.dd[:, 0:n - 1], 1.0))
    sc.wait_ge(sem.ldw, 16)
    sc.activation(T.sq[:, 0:F], T.wb[:], Act.Square, scale=0.5, accum_out=T.land[:, 0:1]).then_inc(sem.sums, 1)
    sc.wait_ge(sem.ldu, 16)
    sc.activation(T.sq[:, F:2 * F], T.ub[:], Act.Square, accum_out=T.land[:, 1:2]).then_inc(sem.sums, 1)

    g.wait_ge(sem.sums, 2)
    left = 0
    if relays:
        _write(g, topo, core, pair, [(k, pair) for k, _ in relays], E_CHIP, sem.handed, sem.sent)
        left += E_CHIP
    if near:
        _write(g, topo, core, pair, [(d, slot(d, core)) for d in near], E_PLANE, sem.arrived, sem.sent)
        left += E_PLANE

    a, rho = T.kr[:, 0:1], T.kr[:, 1:2]
    v.wait_ge(sem.vec, nv[0])
    v.wait_ge(sem.sums, 2)
    vec(v.tensor_scalar(T.gs[:, 0:2], pair, 0.0, None, AluOpType.is_equal))
    v.wait_ge(sem.vec, nv[0])
    vec(v.tensor_tensor(T.gs[:, 2:4], pair, T.gs[:, 0:2], add))
    sc.wait_ge(sem.vec, nv[0])
    sc.activation(T.gs[:, 4:6], T.gs[:, 2:4], Act.Sqrt).then_inc(sem.guess, 1)
    v.wait_ge(sem.vec, nv[0])
    v.wait_ge(sem.guess, 1)
    vec(v.reciprocal(T.iv[:], T.gs[:, 2:6]))
    v.wait_ge(sem.vec, nv[0])
    vec(v.tensor_scalar(a, T.iv[:, 0:1], SHIFT, None, mult))
    vec(v.tensor_scalar(T.dd[:, n - 1:n], T.iv[:, 1:2], SHIFT, None, mult))
    vec(v.tensor_scalar(rho, T.gs[:, 4:5], T.iv[:, 3:4], None, mult))
    sc.wait_ge(sem.vec, nv[0])
    v.wait_ge(sem.vec, nv[0])
    v.wait_ge(sem.ldu, 16)
    vec(v.tensor_scalar(T.ur[:], T.ub[:], rho, None, mult))
    v.wait_ge(sem.vec, nv[0])
    v.wait_ge(sem.ldw, 16)

    due = sum(E_PLANE if core in plan[c][0] else E_RELAY for c in T.cores if c != core)
    big_a, rt, rec = (T.fin[:, i:i + 1] for i in range(3))
    big_b = T.sb[:, n - 1:n]
    sc.wait_ge(sem.arrived, due)
    sc.activation(T.sa[:, 0:n], T.land[:, 0:end:2], Act.Identity, scale=a, accum_out=big_a).then_inc(sem.xk, 1)
    v.wait_ge(sem.arrived, due)
    vec(v.tensor_tensor_scan(T.sb[:, 0:n], T.land[:, 1:end:2], T.dd[:, 0:n], 0.0, add, mult))
    sc.wait_ge(sem.xk, 1)
    sc.wait_ge(sem.vec, nv[0])
    sc.activation(rt, big_b, Act.Sqrt, scale=big_a).then_inc(sem.root, 1)
    v.wait_ge(sem.vec, nv[0])
    vec(v.reciprocal(rec, big_b))
    v.wait_ge(sem.vec, nv[0])
    v.wait_ge(sem.root, 1)
    vec(v.tensor_scalar(T.tp[:], T.ur[:], rt, rec, mult, mult))
    v.wait_ge(sem.vec, nv[0])
    v.tensor_tensor(T.yb[:], T.wb[:], T.tp[:], sub).then_inc(sem.done, 1)
    sy.wait_ge(sem.done, 1)
    sy.dma_start(T.y[:], T.yb[:]).then_inc(sem.stored, 16)
    sy.wait_ge(sem.stored, 16)
    g.wait_ge(sem.sent, left)
